import numpy as np
import ml_dtypes

BF16 = ml_dtypes.bfloat16


def bf(x):
    return np.asarray(x, np.float32).astype(BF16)


def f32(x):
    return np.asarray(x, np.float32)


def f64(x):
    return np.asarray(x).astype(np.float64)


def striped(idx):
    return np.tile(idx.reshape(-1, 16).T, (8, 1))


S, K, M, N, E, Q = 256, 512, 256, 256, 2, 128


def setup_inputs():
    return {"base": bf(np.random.standard_normal((M, S))), "x": bf(np.random.standard_normal((K, N))), "w": bf(np.random.standard_normal((E, K, M)) / np.sqrt(K)), "s": f32(0.5 + np.random.random_sample((M, 1))), "b": f32(0.5 * np.random.standard_normal((M, 1))), "offs": striped(np.random.permutation(S))}


def reference(base, x, w, s, b, offs):
    idx = offs[:16].T.reshape(-1)
    z = f64(base).copy()
    for e in range(E):
        z[:, idx[e * Q : (e + 1) * Q]] += f64(w)[e].T @ f64(x)[:, e * Q : (e + 1) * Q]
    return z * f64(s) + f64(b)

@@ -1,0 +1,63 @@
+import concourse.mybir as mybir
+from concourse.masks import make_identity
+
+BF16, F32, U16 = mybir.dt.bfloat16, mybir.dt.float32, mybir.dt.uint16
+MULT, ADD = mybir.AluOpType.mult, mybir.AluOpType.add
+
+P = 128
+E, K, M, S, N = 2, 512, 256, 256, 256
+PIECE = N // E
+CUT = PIECE // 16
+Q = K // P
+A = M // P
+
+FLOPS = 2 * N * K * M
+BYTES = 2 * (M * S + K * N + E * K * M) + 4 * (M * S + 2 * M) + 2 * P * N // 16
+
+
+def tile_scatter_matmul_kernel(tc, base, x, w, s, b, offs, out):
+    nc = tc.nc
+    with (
+        tc.tile_pool(name="held", bufs=1) as held,
+        tc.psum_pool(name="psum", bufs=1) as psum,
+    ):
+        base_sb = held.tile([P, A, S], BF16)
+        offsets = held.tile([P, N // 16], U16)
+        x_sb = held.tile([P, Q, N], BF16)
+        w_sb = [held.tile([P, Q, M], BF16, name=f"w_sb{e}") for e in range(E)]
+        s_sb = held.tile([P, A], F32)
+        b_sb = held.tile([P, A], F32)
+        out_sb = [held.tile([P, S], F32, name=f"out_sb{a}") for a in range(A)]
+        ident = held.tile([P, P], BF16)
+
+        nc.sync.dma_start(base_sb[:], base.rearrange("(a p) t -> p a t", p=P))
+        nc.sync.dma_start(offsets[:], offs)
+        nc.sync.dma_start(x_sb[:], x.rearrange("(p q) n -> p q n", p=P))
+        for e in range(E):
+            nc.sync.dma_start(w_sb[e][:], w[e].rearrange("(p q) m -> p q m", p=P))
+        nc.sync.dma_start(s_sb[:], s.rearrange("(a p) o -> p (a o)", p=P))
+        nc.sync.dma_start(b_sb[:], b.rearrange("(a p) o -> p (a o)", p=P))
+
+        make_identity(nc, ident[:])
+        windows = [psum.tile([P, S], F32, name=f"window{a}") for a in range(A)]
+        for a in range(A):
+            nc.tensor.matmul(windows[a][:], ident[:], base_sb[:, a, :], start=True, stop=False)
+
+        for e in range(E):
+            places = offsets[:, e * CUT : (e + 1) * CUT]
+            for a in range(A):
+                for q in range(Q):
+                    nc.tensor.matmul(
+                        windows[a][:].indirect(places),
+                        w_sb[e][:, q, a * P : (a + 1) * P],
+                        x_sb[:, q, e * PIECE : (e + 1) * PIECE],
+                        start=False,
+                        stop=(e == E - 1 and q == Q - 1),
+                    )
+
+        out_rows = out.rearrange("(a p) t -> p a t", p=P)
+        for a in range(A):
+            nc.vector.tensor_scalar(
+                out_sb[a][:], windows[a][:], s_sb[:, a : a + 1], b_sb[:, a : a + 1], MULT, ADD
+            )
+            nc.sync.dma_start(out_rows[:, a, :], out_sb[a][:])

@@ -11,6 +11,8 @@ CUT = PIECE // 16
 Q = K // P
 A = M // P
 
+WARM_COLUMNS = 256
+
 FLOPS = 2 * N * K * M
 BYTES = 2 * (M * S + K * N + E * K * M) + 4 * (M * S + 2 * M) + 2 * P * N // 16
 
@@ -30,13 +32,24 @@ def tile_scatter_matmul_kernel(tc, base, x, w, s, b, offs, out):
         out_sb = [held.tile([P, S], F32, name=f"out_sb{a}") for a in range(A)]
         ident = held.tile([P, P], BF16)
 
+        x_rows = x.rearrange("(p q) n -> p q n", p=P)
+        w_rows = w.rearrange("e (p q) m -> e p q m", p=P)
+        halves = (slice(0, Q // 2), slice(Q // 2, Q))
         nc.sync.dma_start(base_sb[:], base.rearrange("(a p) t -> p a t", p=P))
         nc.sync.dma_start(offsets[:], offs)
-        nc.sync.dma_start(x_sb[:], x.rearrange("(p q) n -> p q n", p=P))
-        for e in range(E):
-            nc.sync.dma_start(w_sb[e][:], w[e].rearrange("(p q) m -> p q m", p=P))
+        for half in halves:
+            nc.sync.dma_start(x_sb[:, half, :], x_rows[:, half, :])
+            nc.sync.dma_start(w_sb[0][:, half, :], w_rows[0, :, half, :])
+        for e in range(1, E):
+            nc.sync.dma_start(w_sb[e][:], w_rows[e])
         nc.sync.dma_start(s_sb[:], s.rearrange("(a p) o -> p (a o)", p=P))
         nc.sync.dma_start(b_sb[:], b.rearrange("(a p) o -> p (a o)", p=P))
+
+        zeros = held.tile([P, WARM_COLUMNS], BF16)
+        nc.gpsimd.memset(zeros[:], 0.0)
+        idle_bank = psum.tile([P, WARM_COLUMNS], F32)
+        for i in range(6):
+            nc.tensor.matmul(idle_bank[:], zeros[:, 0:P], zeros[:])
 
         make_identity(nc, ident[:])
         windows = [psum.tile([P, S], F32, name=f"window{a}") for a in range(A)]
@@ -45,15 +58,16 @@ def tile_scatter_matmul_kernel(tc, base, x, w, s, b, offs, out):
 
         for e in range(E):
             places = offsets[:, e * CUT : (e + 1) * CUT]
-            for a in range(A):
-                for q in range(Q):
-                    nc.tensor.matmul(
-                        windows[a][:].indirect(places),
-                        w_sb[e][:, q, a * P : (a + 1) * P],
-                        x_sb[:, q, e * PIECE : (e + 1) * PIECE],
-                        start=False,
-                        stop=(e == E - 1 and q == Q - 1),
-                    )
+            for part in halves if e == 0 else (slice(0, Q),):
+                for a in range(A):
+                    for q in range(part.start, part.stop):
+                        nc.tensor.matmul(
+                            windows[a][:].indirect(places),
+                            w_sb[e][:, q, a * P : (a + 1) * P],
+                            x_sb[:, q, e * PIECE : (e + 1) * PIECE],
+                            start=False,
+                            stop=(e == E - 1 and q == Q - 1),
+                        )
 
         out_rows = out.rearrange("(a p) t -> p a t", p=P)
         for a in range(A):

import concourse.mybir as mybir
from concourse.masks import make_identity

BF16, F32, U16 = mybir.dt.bfloat16, mybir.dt.float32, mybir.dt.uint16
MULT, ADD = mybir.AluOpType.mult, mybir.AluOpType.add

P = 128
E, K, M, S, N = 2, 512, 256, 256, 256
PIECE = N // E
CUT = PIECE // 16
Q = K // P
A = M // P

WARM_COLUMNS = 256

FLOPS = 2 * N * K * M
BYTES = 2 * (M * S + K * N + E * K * M) + 4 * (M * S + 2 * M) + 2 * P * N // 16


def tile_scatter_matmul_kernel(tc, base, x, w, s, b, offs, out):
    nc = tc.nc
    with (
        tc.tile_pool(name="held", bufs=1) as held,
        tc.psum_pool(name="psum", bufs=1) as psum,
    ):
        base_sb = held.tile([P, A, S], BF16)
        offsets = held.tile([P, N // 16], U16)
        x_sb = held.tile([P, Q, N], BF16)
        w_sb = [held.tile([P, Q, M], BF16, name=f"w_sb{e}") for e in range(E)]
        s_sb = held.tile([P, A], F32)
        b_sb = held.tile([P, A], F32)
        out_sb = [held.tile([P, S], F32, name=f"out_sb{a}") for a in range(A)]
        ident = held.tile([P, P], BF16)

        x_rows = x.rearrange("(p q) n -> p q n", p=P)
        w_rows = w.rearrange("e (p q) m -> e p q m", p=P)
        halves = (slice(0, Q // 2), slice(Q // 2, Q))
        nc.sync.dma_start(base_sb[:], base.rearrange("(a p) t -> p a t", p=P))
        nc.sync.dma_start(offsets[:], offs)
        for half in halves:
            nc.sync.dma_start(x_sb[:, half, :], x_rows[:, half, :])
            nc.sync.dma_start(w_sb[0][:, half, :], w_rows[0, :, half, :])
        for e in range(1, E):
            nc.sync.dma_start(w_sb[e][:], w_rows[e])
        nc.sync.dma_start(s_sb[:], s.rearrange("(a p) o -> p (a o)", p=P))
        nc.sync.dma_start(b_sb[:], b.rearrange("(a p) o -> p (a o)", p=P))

        zeros = held.tile([P, WARM_COLUMNS], BF16)
        nc.gpsimd.memset(zeros[:], 0.0)
        idle_bank = psum.tile([P, WARM_COLUMNS], F32)
        for i in range(6):
            nc.tensor.matmul(idle_bank[:], zeros[:, 0:P], zeros[:])

        make_identity(nc, ident[:])
        windows = [psum.tile([P, S], F32, name=f"window{a}") for a in range(A)]
        for a in range(A):
            nc.tensor.matmul(windows[a][:], ident[:], base_sb[:, a, :], start=True, stop=False)

        for e in range(E):
            places = offsets[:, e * CUT : (e + 1) * CUT]
            for part in halves if e == 0 else (slice(0, Q),):
                for a in range(A):
                    for q in range(part.start, part.stop):
                        nc.tensor.matmul(
                            windows[a][:].indirect(places),
                            w_sb[e][:, q, a * P : (a + 1) * P],
                            x_sb[:, q, e * PIECE : (e + 1) * PIECE],
                            start=False,
                            stop=(e == E - 1 and q == Q - 1),
                        )

        out_rows = out.rearrange("(a p) t -> p a t", p=P)
        for a in range(A):
            nc.vector.tensor_scalar(
                out_sb[a][:], windows[a][:], s_sb[:, a : a + 1], b_sb[:, a : a + 1], MULT, ADD
            )
            nc.sync.dma_start(out_rows[:, a, :], out_sb[a][:])
